import numpy as np
import ml_dtypes


def mxq(x, axis, fmt="e4m3"):
    dtype, down = {"e4m3": (ml_dtypes.float8_e4m3fn, 7), "e5m2": (ml_dtypes.float8_e5m2, 14)}[fmt]
    v = np.moveaxis(np.asarray(x, np.float32).astype(ml_dtypes.bfloat16).astype(np.float64), axis, -1)
    blocks = v.reshape(v.shape[:-1] + (-1, 32))
    amax = np.abs(blocks).max(-1, keepdims=True)
    byte = np.maximum(np.where(amax > 0, np.frexp(amax)[1] - 1 + 127, 0) - down, 1)
    scale = np.exp2(byte - 127.0)
    codes = (blocks / scale).astype(np.float32).astype(dtype).astype(np.float64)
    return np.moveaxis((codes * scale).reshape(v.shape), -1, axis)


WIDE = False


def mx_kscale(k):
    if not WIDE:
        return np.ones(k)
    levels = np.array([10, -10, 5, -5, 0])
    if k % 512:
        return np.exp2(np.random.permutation(np.resize(levels, k // 32))).repeat(32)
    a = np.empty((k // 512, 16))
    for p in range(k // 512):
        a[p, :8] = np.random.permutation(np.resize(levels, 8))
        for g in range(8):
            far = levels[np.abs(levels - a[p, g]) >= 10]
            a[p, g + 8] = far[np.random.randint(len(far))]
    return np.exp2(a.ravel()).repeat(32)


def f64(x):
    return np.asarray(x).astype(np.float64)


def striped(idx):
    return np.tile(idx.reshape(-1, 16).T, (8, 1)).astype(np.uint16)


def unstriped(offs):
    return offs[:16].T.reshape(-1).astype(np.int64)


def striped8(idx):
    return np.concatenate([x.reshape(-1, 16).T for x in idx]).astype(np.uint16)


def runs(offs, k):
    lists = np.stack([offs[16 * r : 16 * r + 16].T.reshape(-1) for r in range(8)]).astype(np.int64)
    return lists[np.arange(k) % 512 // 64]


def pack_weight(w):
    k, n = w.shape
    w = f64(np.asarray(w, np.float32).astype(ml_dtypes.bfloat16)).reshape(k // 32, 32, n)
    amax = np.abs(w).max(1)
    byte = np.clip(np.where(amax > 0, np.frexp(amax)[1] - 1 + 127 - 7, 1), 1, 254)
    scaled = (w * np.exp2(127.0 - byte)[:, None, :]).reshape(k, n).astype(np.float32)
    words = np.ascontiguousarray(scaled.reshape(k // 512, 128, 4, n).transpose(0, 1, 3, 2)).astype(ml_dtypes.float8_e4m3fn).view(np.uint8)
    return words, np.ascontiguousarray(byte.astype(np.uint8).reshape(k // 512, 16, n))


def unpack_weight(words, scales):
    g, p, n, _ = words.shape
    vals = np.ascontiguousarray(words).view(ml_dtypes.float8_e4m3fn).astype(np.float64) * np.repeat(np.exp2(scales.astype(np.float64) - 127.0), 8, axis=1)[..., None]
    return vals.transpose(0, 1, 3, 2).reshape(g * 512, n)


K, T, S, N, H = 512, 2048, 512, 512, 512


def setup_inputs():
    n = np.random.standard_normal
    s = mx_kscale(K)[:, None]
    u = mx_kscale(H)
    packed_xT = pack_weight(n((K, T)) * s)
    return {
        "x_words": packed_xT[0],
        "x_scales": packed_xT[1],
        "w1": (n((K, H)) / np.sqrt(K) / s).astype(np.float32),
        "w2": (n((K, H)) / np.sqrt(K) / s).astype(np.float32),
        "gn": (np.random.uniform(0.5, 1.5, (H, 1)) * u[:, None]).astype(np.float32),
        "w3": (n((H, N)) / np.sqrt(H) / u[:, None]).astype(np.float32),
        "offs": striped(np.random.permutation(T)[:S]),
        "hz": striped8(np.random.randint(0, T, (8, S))),
        "n1": striped(np.random.permutation(S)),
        "n2": striped(np.random.permutation(S)),
        "n3": striped(np.random.permutation(S)),
    }


def reference(x_words, x_scales, w1, w2, gn, w3, offs, hz, n1, n2, n3):
    xq = unpack_weight(x_words, x_scales)[:, unstriped(offs)]
    y = mxq(f64(w1), 0, "e4m3").T @ xq
    x_hz = unpack_weight(x_words, x_scales)[np.arange(K)[:, None], runs(hz, K)]
    d = mxq(f64(w2), 0, "e4m3").T @ x_hz
    z = f64(gn) * (y * (np.tanh(d[:, unstriped(n1)] - d[:, unstriped(n2)])))
    h = mxq(f64(w3), 0, "e4m3").T @ mxq(z, 0, "e4m3")
    st = h - h[:, unstriped(n3)]
    return st - (0.5 * st[:, unstriped(n3)])

@@ -1,0 +1,262 @@
+from contextlib import ExitStack
+
+import concourse.mybir as mybir
+
+K, T, S, N, H = 512, 2048, 512, 512, 512
+FLOPS = 2 * (K * H * S * 2 + H * N * S)
+
+F32 = mybir.dt.float32
+BF16 = mybir.dt.bfloat16
+I32 = mybir.dt.int32
+U32 = mybir.dt.uint32
+U16 = mybir.dt.uint16
+U8 = mybir.dt.uint8
+FP8X4 = mybir.dt.float8_e4m3fn_x4
+ACT = mybir.ActivationFunctionType
+ALU = mybir.AluOpType
+
+P = 128
+PACK = 4
+HALF = S // 2
+LANES = 16
+
+
+def tile_picked_twhjointbtwice_none_p_kernel(
+    tc, x_words, x_scales, w1, w2, gn, w3, offs, hz, n1, n2, n3, out
+):
+    nc = tc.nc
+    halves = [slice(0, HALF), slice(HALF, S)]
+
+    def entries(list_tile, cols):
+        return list_tile[:, cols.start // LANES : cols.stop // LANES]
+
+    with ExitStack() as ctx:
+        keep = ctx.enter_context(tc.tile_pool(name="keep", bufs=1))
+        psum = ctx.enter_context(tc.psum_pool(name="psum", bufs=1))
+
+        def load_list(name, src):
+            list_tile = keep.tile([P, S // LANES], U16, name=name)
+            nc.sync.dma_start(list_tile[:], src)
+            return list_tile
+
+        def load_weight_half(name, w, cols):
+            raw = keep.tile([P, PACK, HALF], F32, name=name)
+            nc.sync.dma_start(raw[:], w.rearrange("(p j) c -> p j c", j=PACK)[:, :, cols])
+            return raw
+
+        scale_table = keep.tile([P, T], U8, name="scale_table", tag="scales_then_w1")
+        nc.sync.dma_start(
+            scale_table[:].bitcast(I32),
+            x_scales[0].bitcast(I32).unsqueeze(1).to_broadcast([16, 8, T // 4]),
+        )
+        hz_list = load_list("hz_list", hz)
+        offs_list = load_list("offs_list", offs)
+        n1_list = load_list("n1_list", n1)
+        word_table = keep.tile([P, T], I32, name="word_table", tag="words_then_w3")
+        nc.sync.dma_start(word_table[:], x_words[0].rearrange("p c r -> p (c r)").bitcast(I32))
+        n2_list = load_list("n2_list", n2)
+        n3_list = load_list("n3_list", n3)
+        w2_raw = [load_weight_half(f"w2_raw{a}", w2, cols) for a, cols in enumerate(halves)]
+        gain = keep.tile([P, PACK], F32, name="gain")
+        nc.gpsimd.dma_start(gain[:], gn.rearrange("(p t) o -> p (t o)", t=PACK))
+
+        def pick_scales(name, list_tile, queue):
+            picked = keep.tile([P, S], U8, name=name + "_picked")
+            nc.vector.tensor_copy(picked[:], scale_table[:].indirect(list_tile[:]))
+            plane = keep.tile([P, S], U8, name=name + "_plane", align_bytes=64)
+            nc.vector.tensor_copy(plane[:].bitcast(I32), picked[:].bitcast(I32))
+            for i in range(1, 4):
+                queue.dma_start(plane[i:P:32, :].bitcast(I32), picked[8 * i : P : 32, :].bitcast(I32))
+            return plane
+
+        def pick_words(name, list_tile):
+            words = keep.tile([P, S], U32, name=name, align_bytes=64)
+            nc.vector.tensor_copy(words[:], word_table[:].bitcast(U32).indirect(list_tile[:]))
+            return words
+
+        hz_plane = pick_scales("hz_scales", hz_list, nc.sync)
+        offs_plane = pick_scales("offs_scales", offs_list, nc.sync)
+        w1_raw = keep.tile([P, PACK, H], F32, name="w1_raw", tag="scales_then_w1")
+        nc.sync.dma_start(w1_raw[:], w1.rearrange("(p j) c -> p j c", j=PACK))
+        hz_words = pick_words("hz_words", hz_list)
+        offs_words = pick_words("offs_words", offs_list)
+        w3_raw = keep.tile([P, PACK, N], F32, name="w3_raw", tag="words_then_w3")
+        nc.sync.dma_start(w3_raw[:], w3.rearrange("(p j) c -> p j c", j=PACK))
+
+        def mx_tiles(name, width):
+            rounded = keep.tile([P, width * PACK], BF16, name=name + "_bf16", align_bytes=64)
+            codes = keep.tile([P, width], U32, name=name + "_codes", align_bytes=64)
+            plane = keep.tile([P, width], U8, name=name + "_plane", align_bytes=64)
+            return rounded, codes, plane
+
+        def quantize(operand, cols):
+            rounded, codes, plane = operand
+            nc.vector.quantize_mx(
+                out=codes[:, cols].bitcast(FP8X4),
+                scales=plane[:, cols],
+                in_=rounded[:, cols.start * PACK : cols.stop * PACK],
+            )
+
+        def dealt(rounded):
+            return rounded[:].rearrange("p (t m j) -> p m t j", t=PACK, j=PACK)
+
+        def as_dealt(raw):
+            return raw.rearrange("p j (m t) -> p m t j", t=PACK)
+
+        blocks = [slice(P * t, P * (t + 1)) for t in range(PACK)]
+
+        def product(bank, weight, cols, words, plane):
+            nc.tensor.matmul_mx(
+                out=bank,
+                lhsT=weight[1][:, cols].bitcast(FP8X4),
+                lhsT_scale=weight[2][:, cols],
+                rhs=words.bitcast(FP8X4),
+                rhs_scale=plane,
+                start=True,
+                stop=True,
+            )
+
+        w2_mx = mx_tiles("w2", H)
+        for a, copy in enumerate((nc.scalar.copy, nc.vector.tensor_copy)):
+            copy(dealt(w2_mx[0])[:, 64 * a : 64 * (a + 1)], as_dealt(w2_raw[a][:]))
+        quantize(w2_mx, blocks[0])
+        quantize(w2_mx, slice(P, H))
+        d_banks = []
+        for t in range(PACK):
+            bank = psum.tile([P, S], F32, name=f"d_bank{t}", tag=f"dh{t}")
+            product(bank[:], w2_mx, blocks[t], hz_words[:], hz_plane[:])
+            d_banks.append(bank)
+
+        d_sb = [keep.tile([P, S], F32, name=f"d{t}") for t in range(PACK)]
+        d_n2 = [keep.tile([P, S], F32, name=f"d_n2_{t}") for t in range(PACK)]
+        diff = [keep.tile([P, S], F32, name=f"diff{t}") for t in range(PACK)]
+        gate = [keep.tile([P, S], F32, name=f"gate{t}") for t in range(PACK)]
+        z_planes = keep.tile([P, PACK, S], BF16, name="z_planes")
+        w1_mx = mx_tiles("w1", H)
+        w3_mx = mx_tiles("w3", N)
+        z_mx = mx_tiles("z", S)
+        y_banks = [psum.tile([P, S], F32, name=f"y_bank{t}") for t in range(PACK)]
+
+        def evict_d(t, engine):
+            if engine is nc.vector:
+                nc.vector.tensor_copy(d_sb[t][:], d_banks[t][:])
+            else:
+                nc.scalar.copy(d_sb[t][:], d_banks[t][:])
+
+        def fetch_n2(t, cols):
+            nc.scalar.activation(d_n2[t][:, cols], d_sb[t][:].indirect(entries(n2_list, cols)), ACT.Copy)
+
+        def fetch_n1(t, cols):
+            nc.vector.tensor_tensor(
+                diff[t][:, cols], d_sb[t][:].indirect(entries(n1_list, cols)), d_n2[t][:, cols], ALU.subtract
+            )
+
+        def squash(t, cols):
+            nc.scalar.activation(gate[t][:, cols], diff[t][:, cols], ACT.Tanh)
+
+        def make_z(t, cols):
+            nc.vector.scalar_tensor_tensor(
+                z_planes[:, t, cols], y_banks[t][:, cols], gain[:, t : t + 1], gate[t][:, cols], ALU.mult, ALU.mult
+            )
+
+        def weave(copy, rounded, planes, cols):
+            copy(
+                rounded[:, cols.start * PACK : cols.stop * PACK].rearrange("p (c i j) -> p c j i", i=4, j=PACK),
+                planes[:, :, cols].rearrange("p j (c i) -> p c j i", i=4),
+            )
+
+        h_half = [keep.tile([P, S], F32, name=f"h_half{m}") for m in range(PACK)]
+        h_n3 = [keep.tile([P, S], F32, name=f"h_n3_{m}") for m in range(PACK)]
+        st_neg_half = [keep.tile([P, S], F32, name=f"st_neg_half{m}") for m in range(PACK)]
+        st = [keep.tile([P, S], F32, name=f"st{m}") for m in range(PACK)]
+        result = [keep.tile([P, S], F32, name=f"result{m}") for m in range(PACK)]
+        first, second = halves
+
+        def make_h(m, cols, bank):
+            product(bank[:, cols], w3_mx, blocks[m], z_mx[1][:, cols], z_mx[2][:, cols])
+            nc.scalar.activation(h_half[m][:, cols], bank[:, cols], ACT.Copy, scale=0.5)
+
+        def fetch_h(m, cols):
+            nc.scalar.activation(h_n3[m][:, cols], h_half[m][:].indirect(entries(n3_list, cols)), ACT.Copy)
+
+        def make_st(m, cols):
+            nc.vector.tensor_tensor(st_neg_half[m][:, cols], h_n3[m][:, cols], h_half[m][:, cols], ALU.subtract)
+
+        def finish_on_vector(m, cols):
+            nc.vector.tensor_tensor(
+                result[m][:, cols], st_neg_half[m][:].indirect(entries(n3_list, cols)), st[m][:, cols], ALU.add
+            )
+            nc.sync.dma_start(out[blocks[m], cols], result[m][:, cols])
+
+        def finish_with_scalar(m, cols):
+            nc.scalar.activation(st[m][:, cols], st_neg_half[m][:].indirect(entries(n3_list, cols)), ACT.Copy)
+            nc.vector.scalar_tensor_tensor(
+                result[m][:, cols], st_neg_half[m][:, cols], -2.0, st[m][:, cols], ALU.mult, ALU.add
+            )
+            nc.sync.dma_start(out[blocks[m], cols], result[m][:, cols])
+
+        evict_d(0, nc.scalar)
+        evict_d(1, nc.vector)
+        fetch_n2(0, first)
+        fetch_n2(1, first)
+        evict_d(2, nc.scalar)
+        fetch_n2(2, first)
+        evict_d(3, nc.scalar)
+        fetch_n2(3, first)
+        nc.vector.tensor_copy(dealt(w1_mx[0]), as_dealt(w1_raw[:]))
+        fetch_n1(0, first)
+        quantize(w1_mx, slice(0, H))
+        for t in range(PACK):
+            product(y_banks[t][:], w1_mx, blocks[t], offs_words[:], offs_plane[:])
+        for t in range(1, PACK):
+            fetch_n1(t, first)
+        squash(0, first)
+        squash(1, first)
+        make_z(0, first)
+        make_z(1, first)
+        fetch_n2(0, second)
+        squash(2, first)
+        squash(3, first)
+        fetch_n1(0, second)
+        make_z(2, first)
+        make_z(3, first)
+        fetch_n2(1, second)
+        squash(0, second)
+        fetch_n1(1, second)
+        weave(nc.vector.tensor_copy, z_mx[0], z_planes, first)
+        fetch_n2(2, second)
+        fetch_n2(3, second)
+        squash(1, second)
+        fetch_n1(2, second)
+        quantize(z_mx, first)
+        make_z(0, second)
+        fetch_n1(3, second)
+        weave(nc.scalar.copy, w3_mx[0], w3_raw, first)
+        squash(2, second)
+        squash(3, second)
+        make_z(1, second)
+        quantize(w3_mx, first)
+        make_z(2, second)
+        make_z(3, second)
+        weave(nc.scalar.copy, w3_mx[0], w3_raw, second)
+        h_banks = [psum.tile([P, S], F32, name=f"h_bank{m}", tag=f"dh{m}") for m in range(PACK)]
+        make_h(0, first, h_banks[0])
+        weave(nc.vector.tensor_copy, z_mx[0], z_planes, second)
+        quantize(z_mx, second)
+        quantize(w3_mx, second)
+        make_h(0, second, h_banks[0])
+        for m in range(PACK):
+            for cols in halves:
+                fetch_h(m, cols)
+            if m + 1 < PACK:
+                make_h(m + 1, slice(0, S), h_banks[m + 1])
+            for cols in halves if m in (0, PACK - 1) else [slice(0, S)]:
+                make_st(m, cols)
+            if m < 2:
+                nc.vector.tensor_scalar(st[m][:], st_neg_half[m][:], -2.0, None, ALU.mult)
+                for cols in halves:
+                    finish_on_vector(m, cols)
+            else:
+                nc.vector.tensor_scalar(st[m][:, first], st_neg_half[m][:, first], -2.0, None, ALU.mult)
+                finish_on_vector(m, first)
+                finish_with_scalar(m, second)

@@ -19,6 +19,7 @@ P = 128
 PACK = 4
 HALF = S // 2
 LANES = 16
+WINDOW = S + 32
 
 
 def tile_picked_twhjointbtwice_none_p_kernel(
@@ -40,11 +41,11 @@ def tile_picked_twhjointbtwice_none_p_kernel(
             return list_tile
 
         def load_weight_half(name, w, cols):
-            raw = keep.tile([P, PACK, HALF], F32, name=name)
+            raw = keep.tile([P, PACK, HALF], F32, name=name, align_bytes=64)
             nc.sync.dma_start(raw[:], w.rearrange("(p j) c -> p j c", j=PACK)[:, :, cols])
             return raw
 
-        scale_table = keep.tile([P, T], U8, name="scale_table", tag="scales_then_w1")
+        scale_table = keep.tile([P, T], U8, name="scale_table", align_bytes=64)
         nc.sync.dma_start(
             scale_table[:].bitcast(I32),
             x_scales[0].bitcast(I32).unsqueeze(1).to_broadcast([16, 8, T // 4]),
@@ -58,33 +59,34 @@ def tile_picked_twhjointbtwice_none_p_kernel(
         n3_list = load_list("n3_list", n3)
         w2_raw = [load_weight_half(f"w2_raw{a}", w2, cols) for a, cols in enumerate(halves)]
         gain = keep.tile([P, PACK], F32, name="gain")
-        nc.gpsimd.dma_start(gain[:], gn.rearrange("(p t) o -> p (t o)", t=PACK))
+        nc.scalar.dma_start(gain[:], gn.rearrange("(p t) o -> p (t o)", t=PACK))
 
-        def pick_scales(name, list_tile, queue):
-            picked = keep.tile([P, S], U8, name=name + "_picked")
+        def pick_scales(name, list_tile):
+            picked = keep.tile([P, S], U8, name=name)
             nc.vector.tensor_copy(picked[:], scale_table[:].indirect(list_tile[:]))
-            plane = keep.tile([P, S], U8, name=name + "_plane", align_bytes=64)
-            nc.vector.tensor_copy(plane[:].bitcast(I32), picked[:].bitcast(I32))
-            for i in range(1, 4):
-                queue.dma_start(plane[i:P:32, :].bitcast(I32), picked[8 * i : P : 32, :].bitcast(I32))
+            return picked
+
+        def place_scales(name, picked):
+            plane = keep.tile([P, S], U8, name=name, align_bytes=64)
+            nc.gpsimd.memset(plane[:], 0)
+            for i in range(4):
+                nc.sync.dma_start(plane[i:P:32, :].bitcast(I32), picked[8 * i : P : 32, :].bitcast(I32))
             return plane
 
-        def pick_words(name, list_tile):
-            words = keep.tile([P, S], U32, name=name, align_bytes=64)
+        def pick_words(name, list_tile, tag):
+            words = keep.tile([P, S], U32, name=name, tag=tag, align_bytes=64)
             nc.vector.tensor_copy(words[:], word_table[:].bitcast(U32).indirect(list_tile[:]))
             return words
 
-        hz_plane = pick_scales("hz_scales", hz_list, nc.sync)
-        offs_plane = pick_scales("offs_scales", offs_list, nc.sync)
-        w1_raw = keep.tile([P, PACK, H], F32, name="w1_raw", tag="scales_then_w1")
+        hz_plane = place_scales("hz_plane", pick_scales("hz_scales", hz_list))
+        offs_scales = pick_scales("offs_scales", offs_list)
+        w1_raw = keep.tile([P, PACK, H], F32, name="w1_raw", tag="scale_table", align_bytes=64)
         nc.sync.dma_start(w1_raw[:], w1.rearrange("(p j) c -> p j c", j=PACK))
-        hz_words = pick_words("hz_words", hz_list)
-        offs_words = pick_words("offs_words", offs_list)
-        w3_raw = keep.tile([P, PACK, N], F32, name="w3_raw", tag="words_then_w3")
-        nc.sync.dma_start(w3_raw[:], w3.rearrange("(p j) c -> p j c", j=PACK))
+        offs_plane = place_scales("offs_plane", offs_scales)
+        hz_words = pick_words("hz_words", hz_list, "hz_words")
 
-        def mx_tiles(name, width):
-            rounded = keep.tile([P, width * PACK], BF16, name=name + "_bf16", align_bytes=64)
+        def mx_tiles(name, width, tag=None):
+            rounded = keep.tile([P, width * PACK], BF16, name=name + "_bf16", tag=tag or name, align_bytes=64)
             codes = keep.tile([P, width], U32, name=name + "_codes", align_bytes=64)
             plane = keep.tile([P, width], U8, name=name + "_plane", align_bytes=64)
             return rounded, codes, plane
@@ -126,29 +128,44 @@ def tile_picked_twhjointbtwice_none_p_kernel(
             bank = psum.tile([P, S], F32, name=f"d_bank{t}", tag=f"dh{t}")
             product(bank[:], w2_mx, blocks[t], hz_words[:], hz_plane[:])
             d_banks.append(bank)
+        offs_words = pick_words("offs_words", offs_list, "w2")
+        w3_raw = keep.tile([P, PACK, N], F32, name="w3_raw", tag="words_then_w3")
+        nc.sync.dma_start(w3_raw[:], w3.rearrange("(p j) c -> p j c", j=PACK))
 
-        d_sb = [keep.tile([P, S], F32, name=f"d{t}") for t in range(PACK)]
-        d_n2 = [keep.tile([P, S], F32, name=f"d_n2_{t}") for t in range(PACK)]
-        diff = [keep.tile([P, S], F32, name=f"diff{t}") for t in range(PACK)]
+        def windows(name, count=PACK):
+            tiles = [keep.tile([P, WINDOW], F32, name=f"{name}{t}") for t in range(count)]
+            for tile in tiles:
+                nc.gpsimd.memset(tile[:, S:], 0.0)
+            return tiles
+
+        d_sb = windows("d", 3)
+        d_sb.append(d_sb[0])
+        d_n2 = {}
+        ring = ["ring0", "ring1", "scale_table"]
+        diff = {}
         gate = [keep.tile([P, S], F32, name=f"gate{t}") for t in range(PACK)]
-        z_planes = keep.tile([P, PACK, S], BF16, name="z_planes")
+        z_planes = keep.tile([P, PACK, S], BF16, name="z_planes", align_bytes=64)
         w1_mx = mx_tiles("w1", H)
-        w3_mx = mx_tiles("w3", N)
         z_mx = mx_tiles("z", S)
         y_banks = [psum.tile([P, S], F32, name=f"y_bank{t}") for t in range(PACK)]
 
         def evict_d(t, engine):
             if engine is nc.vector:
-                nc.vector.tensor_copy(d_sb[t][:], d_banks[t][:])
+                nc.vector.tensor_copy(d_sb[t][:, :S], d_banks[t][:])
             else:
-                nc.scalar.copy(d_sb[t][:], d_banks[t][:])
+                nc.scalar.copy(d_sb[t][:, :S], d_banks[t][:])
 
         def fetch_n2(t, cols):
-            nc.scalar.activation(d_n2[t][:, cols], d_sb[t][:].indirect(entries(n2_list, cols)), ACT.Copy)
+            if t not in d_n2:
+                d_n2[t] = keep.tile([P, S], F32, name=f"d_n2_{t}", tag=ring[t % 3], align_bytes=64)
+            nc.scalar.activation(d_n2[t][:, cols], d_sb[t][:].indirect(entries(n2_list, cols)), ACT.Copy, scale=-1.0)
 
         def fetch_n1(t, cols):
+            if t not in diff:
+                tag = ring[(t + 2) % 3]
+                diff[t] = keep.tile([P, S], F32, name=f"diff{t}", tag=tag, align_bytes=64)
             nc.vector.tensor_tensor(
-                diff[t][:, cols], d_sb[t][:].indirect(entries(n1_list, cols)), d_n2[t][:, cols], ALU.subtract
+                diff[t][:, cols], d_sb[t][:].indirect(entries(n1_list, cols)), d_n2[t][:, cols], ALU.add
             )
 
         def squash(t, cols):
@@ -165,19 +182,31 @@ def tile_picked_twhjointbtwice_none_p_kernel(
                 planes[:, :, cols].rearrange("p j (c i) -> p c j i", i=4),
             )
 
-        h_half = [keep.tile([P, S], F32, name=f"h_half{m}") for m in range(PACK)]
+        h_half = windows("h_half")
         h_n3 = [keep.tile([P, S], F32, name=f"h_n3_{m}") for m in range(PACK)]
-        st_neg_half = [keep.tile([P, S], F32, name=f"st_neg_half{m}") for m in range(PACK)]
+        st_neg_half = windows("st_neg_half")
         st = [keep.tile([P, S], F32, name=f"st{m}") for m in range(PACK)]
         result = [keep.tile([P, S], F32, name=f"result{m}") for m in range(PACK)]
         first, second = halves
+        whole = slice(0, S)
 
-        def make_h(m, cols, bank):
-            product(bank[:, cols], w3_mx, blocks[m], z_mx[1][:, cols], z_mx[2][:, cols])
-            nc.scalar.activation(h_half[m][:, cols], bank[:, cols], ACT.Copy, scale=0.5)
+        def make_h(m, cols):
+            product(h_banks[m][:, cols], w3_mx, blocks[m], z_mx[1][:, cols], z_mx[2][:, cols])
+
+        def evict_h(m, cols):
+            nc.scalar.activation(h_half[m][:, cols], h_banks[m][:, cols], ACT.Copy, scale=0.5)
+
+        def evict_h_on_vector(m, cols):
+            nc.vector.tensor_scalar(h_half[m][:, cols], h_banks[m][:, cols], 0.5, None, ALU.mult)
 
         def fetch_h(m, cols):
             nc.scalar.activation(h_n3[m][:, cols], h_half[m][:].indirect(entries(n3_list, cols)), ACT.Copy)
+
+        def fetch_h_on_vector(m, cols):
+            nc.vector.tensor_copy(h_n3[m][:, cols], h_half[m][:].indirect(entries(n3_list, cols)))
+
+        def double(m, cols):
+            nc.vector.tensor_scalar(st[m][:, cols], st_neg_half[m][:, cols], -2.0, None, ALU.mult)
 
         def make_st(m, cols):
             nc.vector.tensor_tensor(st_neg_half[m][:, cols], h_n3[m][:, cols], h_half[m][:, cols], ALU.subtract)
@@ -195,68 +224,67 @@ def tile_picked_twhjointbtwice_none_p_kernel(
             )
             nc.sync.dma_start(out[blocks[m], cols], result[m][:, cols])
 
+        last = PACK - 1
         evict_d(0, nc.scalar)
-        evict_d(1, nc.vector)
-        fetch_n2(0, first)
-        fetch_n2(1, first)
-        evict_d(2, nc.scalar)
-        fetch_n2(2, first)
-        evict_d(3, nc.scalar)
-        fetch_n2(3, first)
+        fetch_n2(0, whole)
         nc.vector.tensor_copy(dealt(w1_mx[0]), as_dealt(w1_raw[:]))
-        fetch_n1(0, first)
-        quantize(w1_mx, slice(0, H))
+        evict_d(1, nc.scalar)
+        fetch_n1(0, whole)
+        fetch_n2(1, whole)
+        quantize(w1_mx, whole)
         for t in range(PACK):
             product(y_banks[t][:], w1_mx, blocks[t], offs_words[:], offs_plane[:])
-        for t in range(1, PACK):
-            fetch_n1(t, first)
-        squash(0, first)
-        squash(1, first)
-        make_z(0, first)
-        make_z(1, first)
-        fetch_n2(0, second)
-        squash(2, first)
-        squash(3, first)
-        fetch_n1(0, second)
-        make_z(2, first)
-        make_z(3, first)
-        fetch_n2(1, second)
-        squash(0, second)
-        fetch_n1(1, second)
-        weave(nc.vector.tensor_copy, z_mx[0], z_planes, first)
-        fetch_n2(2, second)
-        fetch_n2(3, second)
-        squash(1, second)
-        fetch_n1(2, second)
-        quantize(z_mx, first)
-        make_z(0, second)
-        fetch_n1(3, second)
+        evict_d(2, nc.scalar)
+        squash(0, whole)
+        fetch_n1(1, whole)
+        fetch_n2(2, whole)
+        make_z(0, whole)
+        evict_d(3, nc.scalar)
+        squash(1, whole)
+        fetch_n1(2, whole)
+        fetch_n2(last, first)
+        fetch_n2(last, second)
+        make_z(1, whole)
+        squash(2, whole)
+        fetch_n1(last, first)
+        fetch_n1(last, second)
+        make_z(2, whole)
+        squash(last, first)
+        squash(last, second)
+        w3_mx = mx_tiles("w3", N, ring[(last + 2) % 3])
         weave(nc.scalar.copy, w3_mx[0], w3_raw, first)
-        squash(2, second)
-        squash(3, second)
-        make_z(1, second)
-        quantize(w3_mx, first)
-        make_z(2, second)
-        make_z(3, second)
         weave(nc.scalar.copy, w3_mx[0], w3_raw, second)
-        h_banks = [psum.tile([P, S], F32, name=f"h_bank{m}", tag=f"dh{m}") for m in range(PACK)]
-        make_h(0, first, h_banks[0])
+        make_z(last, first)
+        make_z(last, second)
+        weave(nc.vector.tensor_copy, z_mx[0], z_planes, first)
         weave(nc.vector.tensor_copy, z_mx[0], z_planes, second)
-        quantize(z_mx, second)
+        quantize(w3_mx, first)
+        quantize(z_mx, whole)
+        h_banks = [psum.tile([P, S], F32, name=f"h_bank{m}", tag=f"dh{m}") for m in range(PACK)]
+        make_h(0, whole)
+        make_h(1, whole)
         quantize(w3_mx, second)
-        make_h(0, second, h_banks[0])
-        for m in range(PACK):
-            for cols in halves:
-                fetch_h(m, cols)
-            if m + 1 < PACK:
-                make_h(m + 1, slice(0, S), h_banks[m + 1])
-            for cols in halves if m in (0, PACK - 1) else [slice(0, S)]:
-                make_st(m, cols)
-            if m < 2:
-                nc.vector.tensor_scalar(st[m][:], st_neg_half[m][:], -2.0, None, ALU.mult)
-                for cols in halves:
-                    finish_on_vector(m, cols)
-            else:
-                nc.vector.tensor_scalar(st[m][:, first], st_neg_half[m][:, first], -2.0, None, ALU.mult)
-                finish_on_vector(m, first)
-                finish_with_scalar(m, second)
+        make_h(2, whole)
+        make_h(3, whole)
+        evict_h_on_vector(0, whole)
+        evict_h(1, whole)
+        fetch_h_on_vector(0, first)
+        fetch_h_on_vector(0, second)
+        fetch_h(1, whole)
+        make_st(0, whole)
+        evict_h(2, whole)
+        make_st(1, whole)
+        double(0, whole)
+        fetch_h(2, whole)
+        double(1, first)
+        finish_on_vector(0, whole)
+        finish_with_scalar(1, second)
+        evict_h(3, whole)
+        make_st(2, whole)
+        finish_on_vector(1, first)
+        fetch_h(3, whole)
+        finish_with_scalar(2, whole)
+        make_st(3, whole)
+        double(3, first)
+        finish_with_scalar(3, second)
+        finish_on_vector(3, first)

@@ -119,8 +119,8 @@ def tile_picked_twhjointbtwice_none_p_kernel(
             )
 
         w2_mx = mx_tiles("w2", H)
-        for a, copy in enumerate((nc.scalar.copy, nc.vector.tensor_copy)):
-            copy(dealt(w2_mx[0])[:, 64 * a : 64 * (a + 1)], as_dealt(w2_raw[a][:]))
+        for a in range(2):
+            nc.vector.tensor_copy(dealt(w2_mx[0])[:, 64 * a : 64 * (a + 1)], as_dealt(w2_raw[a][:]))
         quantize(w2_mx, blocks[0])
         quantize(w2_mx, slice(P, H))
         d_banks = []
@@ -141,7 +141,7 @@ def tile_picked_twhjointbtwice_none_p_kernel(
         d_sb = windows("d", 3)
         d_sb.append(d_sb[0])
         d_n2 = {}
-        ring = ["ring0", "ring1", "scale_table"]
+        ring = ["ring0", "ring1", "w1"]
         diff = {}
         gate = [keep.tile([P, S], F32, name=f"gate{t}") for t in range(PACK)]
         z_planes = keep.tile([P, PACK, S], BF16, name="z_planes", align_bytes=64)
@@ -190,14 +190,22 @@ def tile_picked_twhjointbtwice_none_p_kernel(
         first, second = halves
         whole = slice(0, S)
 
+        h_banks = {}
+
+        def h_bank(m, cols):
+            if (m, cols.start) not in h_banks:
+                tag = f"y_bank{m}" if cols.start else f"dh{m}"
+                h_banks[m, cols.start] = psum.tile([P, cols.stop - cols.start], F32, name=f"h{m}_{cols.start}", tag=tag)
+            return h_banks[m, cols.start][:]
+
         def make_h(m, cols):
-            product(h_banks[m][:, cols], w3_mx, blocks[m], z_mx[1][:, cols], z_mx[2][:, cols])
+            product(h_bank(m, cols), w3_mx, blocks[m], z_mx[1][:, cols], z_mx[2][:, cols])
 
         def evict_h(m, cols):
-            nc.scalar.activation(h_half[m][:, cols], h_banks[m][:, cols], ACT.Copy, scale=0.5)
+            nc.scalar.activation(h_half[m][:, cols], h_bank(m, cols), ACT.Copy, scale=0.5)
 
         def evict_h_on_vector(m, cols):
-            nc.vector.tensor_scalar(h_half[m][:, cols], h_banks[m][:, cols], 0.5, None, ALU.mult)
+            nc.vector.tensor_scalar(h_half[m][:, cols], h_bank(m, cols), 0.5, None, ALU.mult)
 
         def fetch_h(m, cols):
             nc.scalar.activation(h_n3[m][:, cols], h_half[m][:].indirect(entries(n3_list, cols)), ACT.Copy)
@@ -229,11 +237,11 @@ def tile_picked_twhjointbtwice_none_p_kernel(
         fetch_n2(0, whole)
         nc.vector.tensor_copy(dealt(w1_mx[0]), as_dealt(w1_raw[:]))
         evict_d(1, nc.scalar)
-        fetch_n1(0, whole)
-        fetch_n2(1, whole)
         quantize(w1_mx, whole)
         for t in range(PACK):
             product(y_banks[t][:], w1_mx, blocks[t], offs_words[:], offs_plane[:])
+        fetch_n1(0, whole)
+        fetch_n2(1, whole)
         evict_d(2, nc.scalar)
         squash(0, whole)
         fetch_n1(1, whole)
@@ -253,38 +261,45 @@ def tile_picked_twhjointbtwice_none_p_kernel(
         squash(last, second)
         w3_mx = mx_tiles("w3", N, ring[(last + 2) % 3])
         weave(nc.scalar.copy, w3_mx[0], w3_raw, first)
-        weave(nc.scalar.copy, w3_mx[0], w3_raw, second)
         make_z(last, first)
         make_z(last, second)
+        weave(nc.scalar.copy, z_mx[0], z_planes, slice(384, S))
+        weave(nc.scalar.copy, w3_mx[0], w3_raw, second)
         weave(nc.vector.tensor_copy, z_mx[0], z_planes, first)
-        weave(nc.vector.tensor_copy, z_mx[0], z_planes, second)
         quantize(w3_mx, first)
-        quantize(z_mx, whole)
-        h_banks = [psum.tile([P, S], F32, name=f"h_bank{m}", tag=f"dh{m}") for m in range(PACK)]
-        make_h(0, whole)
-        make_h(1, whole)
+        quantize(z_mx, first)
+        make_h(0, first)
+        make_h(1, first)
+        weave(nc.vector.tensor_copy, z_mx[0], z_planes, slice(HALF, 384))
+        quantize(z_mx, second)
+        make_h(0, second)
+        make_h(1, second)
+        evict_h(0, first)
+        evict_h(1, first)
+        evict_h_on_vector(0, second)
         quantize(w3_mx, second)
         make_h(2, whole)
         make_h(3, whole)
-        evict_h_on_vector(0, whole)
-        evict_h(1, whole)
-        fetch_h_on_vector(0, first)
-        fetch_h_on_vector(0, second)
+        evict_h(1, second)
+        for cols in halves:
+            fetch_h_on_vector(0, cols)
         fetch_h(1, whole)
-        make_st(0, whole)
+        for cols in halves:
+            make_st(0, cols)
         evict_h(2, whole)
-        make_st(1, whole)
-        double(0, whole)
-        fetch_h(2, whole)
-        double(1, first)
-        finish_on_vector(0, whole)
-        finish_with_scalar(1, second)
         evict_h(3, whole)
+        for cols in halves:
+            double(0, cols)
+        fetch_h(2, whole)
+        fetch_h(3, whole)
+        finish_on_vector(0, first)
+        make_st(1, whole)
+        finish_on_vector(0, second)
+        double(1, whole)
         make_st(2, whole)
         finish_on_vector(1, first)
-        fetch_h(3, whole)
-        finish_with_scalar(2, whole)
         make_st(3, whole)
-        double(3, first)
+        finish_with_scalar(2, whole)
+        finish_on_vector(1, second)
+        finish_with_scalar(3, first)
         finish_with_scalar(3, second)
-        finish_on_vector(3, first)

from contextlib import ExitStack

import concourse.mybir as mybir

K, T, S, N, H = 512, 2048, 512, 512, 512
FLOPS = 2 * (K * H * S * 2 + H * N * S)

F32 = mybir.dt.float32
BF16 = mybir.dt.bfloat16
I32 = mybir.dt.int32
U32 = mybir.dt.uint32
U16 = mybir.dt.uint16
U8 = mybir.dt.uint8
FP8X4 = mybir.dt.float8_e4m3fn_x4
ACT = mybir.ActivationFunctionType
ALU = mybir.AluOpType

P = 128
PACK = 4
HALF = S // 2
LANES = 16
WINDOW = S + 32


def tile_picked_twhjointbtwice_none_p_kernel(
    tc, x_words, x_scales, w1, w2, gn, w3, offs, hz, n1, n2, n3, out
):
    nc = tc.nc
    halves = [slice(0, HALF), slice(HALF, S)]

    def entries(list_tile, cols):
        return list_tile[:, cols.start // LANES : cols.stop // LANES]

    with ExitStack() as ctx:
        keep = ctx.enter_context(tc.tile_pool(name="keep", bufs=1))
        psum = ctx.enter_context(tc.psum_pool(name="psum", bufs=1))

        def load_list(name, src):
            list_tile = keep.tile([P, S // LANES], U16, name=name)
            nc.sync.dma_start(list_tile[:], src)
            return list_tile

        def load_weight_half(name, w, cols):
            raw = keep.tile([P, PACK, HALF], F32, name=name, align_bytes=64)
            nc.sync.dma_start(raw[:], w.rearrange("(p j) c -> p j c", j=PACK)[:, :, cols])
            return raw

        scale_table = keep.tile([P, T], U8, name="scale_table", align_bytes=64)
        nc.sync.dma_start(
            scale_table[:].bitcast(I32),
            x_scales[0].bitcast(I32).unsqueeze(1).to_broadcast([16, 8, T // 4]),
        )
        hz_list = load_list("hz_list", hz)
        offs_list = load_list("offs_list", offs)
        n1_list = load_list("n1_list", n1)
        word_table = keep.tile([P, T], I32, name="word_table", tag="words_then_w3")
        nc.sync.dma_start(word_table[:], x_words[0].rearrange("p c r -> p (c r)").bitcast(I32))
        n2_list = load_list("n2_list", n2)
        n3_list = load_list("n3_list", n3)
        w2_raw = [load_weight_half(f"w2_raw{a}", w2, cols) for a, cols in enumerate(halves)]
        gain = keep.tile([P, PACK], F32, name="gain")
        nc.scalar.dma_start(gain[:], gn.rearrange("(p t) o -> p (t o)", t=PACK))

        def pick_scales(name, list_tile):
            picked = keep.tile([P, S], U8, name=name)
            nc.vector.tensor_copy(picked[:], scale_table[:].indirect(list_tile[:]))
            return picked

        def place_scales(name, picked):
            plane = keep.tile([P, S], U8, name=name, align_bytes=64)
            nc.gpsimd.memset(plane[:], 0)
            for i in range(4):
                nc.sync.dma_start(plane[i:P:32, :].bitcast(I32), picked[8 * i : P : 32, :].bitcast(I32))
            return plane

        def pick_words(name, list_tile, tag):
            words = keep.tile([P, S], U32, name=name, tag=tag, align_bytes=64)
            nc.vector.tensor_copy(words[:], word_table[:].bitcast(U32).indirect(list_tile[:]))
            return words

        hz_plane = place_scales("hz_plane", pick_scales("hz_scales", hz_list))
        offs_scales = pick_scales("offs_scales", offs_list)
        w1_raw = keep.tile([P, PACK, H], F32, name="w1_raw", tag="scale_table", align_bytes=64)
        nc.sync.dma_start(w1_raw[:], w1.rearrange("(p j) c -> p j c", j=PACK))
        offs_plane = place_scales("offs_plane", offs_scales)
        hz_words = pick_words("hz_words", hz_list, "hz_words")

        def mx_tiles(name, width, tag=None):
            rounded = keep.tile([P, width * PACK], BF16, name=name + "_bf16", tag=tag or name, align_bytes=64)
            codes = keep.tile([P, width], U32, name=name + "_codes", align_bytes=64)
            plane = keep.tile([P, width], U8, name=name + "_plane", align_bytes=64)
            return rounded, codes, plane

        def quantize(operand, cols):
            rounded, codes, plane = operand
            nc.vector.quantize_mx(
                out=codes[:, cols].bitcast(FP8X4),
                scales=plane[:, cols],
                in_=rounded[:, cols.start * PACK : cols.stop * PACK],
            )

        def dealt(rounded):
            return rounded[:].rearrange("p (t m j) -> p m t j", t=PACK, j=PACK)

        def as_dealt(raw):
            return raw.rearrange("p j (m t) -> p m t j", t=PACK)

        blocks = [slice(P * t, P * (t + 1)) for t in range(PACK)]

        def product(bank, weight, cols, words, plane):
            nc.tensor.matmul_mx(
                out=bank,
                lhsT=weight[1][:, cols].bitcast(FP8X4),
                lhsT_scale=weight[2][:, cols],
                rhs=words.bitcast(FP8X4),
                rhs_scale=plane,
                start=True,
                stop=True,
            )

        w2_mx = mx_tiles("w2", H)
        for a in range(2):
            nc.vector.tensor_copy(dealt(w2_mx[0])[:, 64 * a : 64 * (a + 1)], as_dealt(w2_raw[a][:]))
        quantize(w2_mx, blocks[0])
        quantize(w2_mx, slice(P, H))
        d_banks = []
        for t in range(PACK):
            bank = psum.tile([P, S], F32, name=f"d_bank{t}", tag=f"dh{t}")
            product(bank[:], w2_mx, blocks[t], hz_words[:], hz_plane[:])
            d_banks.append(bank)
        offs_words = pick_words("offs_words", offs_list, "w2")
        w3_raw = keep.tile([P, PACK, N], F32, name="w3_raw", tag="words_then_w3")
        nc.sync.dma_start(w3_raw[:], w3.rearrange("(p j) c -> p j c", j=PACK))

        def windows(name, count=PACK):
            tiles = [keep.tile([P, WINDOW], F32, name=f"{name}{t}") for t in range(count)]
            for tile in tiles:
                nc.gpsimd.memset(tile[:, S:], 0.0)
            return tiles

        d_sb = windows("d", 3)
        d_sb.append(d_sb[0])
        d_n2 = {}
        ring = ["ring0", "ring1", "w1"]
        diff = {}
        gate = [keep.tile([P, S], F32, name=f"gate{t}") for t in range(PACK)]
        z_planes = keep.tile([P, PACK, S], BF16, name="z_planes", align_bytes=64)
        w1_mx = mx_tiles("w1", H)
        z_mx = mx_tiles("z", S)
        y_banks = [psum.tile([P, S], F32, name=f"y_bank{t}") for t in range(PACK)]

        def evict_d(t, engine):
            if engine is nc.vector:
                nc.vector.tensor_copy(d_sb[t][:, :S], d_banks[t][:])
            else:
                nc.scalar.copy(d_sb[t][:, :S], d_banks[t][:])

        def fetch_n2(t, cols):
            if t not in d_n2:
                d_n2[t] = keep.tile([P, S], F32, name=f"d_n2_{t}", tag=ring[t % 3], align_bytes=64)
            nc.scalar.activation(d_n2[t][:, cols], d_sb[t][:].indirect(entries(n2_list, cols)), ACT.Copy, scale=-1.0)

        def fetch_n1(t, cols):
            if t not in diff:
                tag = ring[(t + 2) % 3]
                diff[t] = keep.tile([P, S], F32, name=f"diff{t}", tag=tag, align_bytes=64)
            nc.vector.tensor_tensor(
                diff[t][:, cols], d_sb[t][:].indirect(entries(n1_list, cols)), d_n2[t][:, cols], ALU.add
            )

        def squash(t, cols):
            nc.scalar.activation(gate[t][:, cols], diff[t][:, cols], ACT.Tanh)

        def make_z(t, cols):
            nc.vector.scalar_tensor_tensor(
                z_planes[:, t, cols], y_banks[t][:, cols], gain[:, t : t + 1], gate[t][:, cols], ALU.mult, ALU.mult
            )

        def weave(copy, rounded, planes, cols):
            copy(
                rounded[:, cols.start * PACK : cols.stop * PACK].rearrange("p (c i j) -> p c j i", i=4, j=PACK),
                planes[:, :, cols].rearrange("p j (c i) -> p c j i", i=4),
            )

        h_half = windows("h_half")
        h_n3 = [keep.tile([P, S], F32, name=f"h_n3_{m}") for m in range(PACK)]
        st_neg_half = windows("st_neg_half")
        st = [keep.tile([P, S], F32, name=f"st{m}") for m in range(PACK)]
        result = [keep.tile([P, S], F32, name=f"result{m}") for m in range(PACK)]
        first, second = halves
        whole = slice(0, S)

        h_banks = {}

        def h_bank(m, cols):
            if (m, cols.start) not in h_banks:
                tag = f"y_bank{m}" if cols.start else f"dh{m}"
                h_banks[m, cols.start] = psum.tile([P, cols.stop - cols.start], F32, name=f"h{m}_{cols.start}", tag=tag)
            return h_banks[m, cols.start][:]

        def make_h(m, cols):
            product(h_bank(m, cols), w3_mx, blocks[m], z_mx[1][:, cols], z_mx[2][:, cols])

        def evict_h(m, cols):
            nc.scalar.activation(h_half[m][:, cols], h_bank(m, cols), ACT.Copy, scale=0.5)

        def evict_h_on_vector(m, cols):
            nc.vector.tensor_scalar(h_half[m][:, cols], h_bank(m, cols), 0.5, None, ALU.mult)

        def fetch_h(m, cols):
            nc.scalar.activation(h_n3[m][:, cols], h_half[m][:].indirect(entries(n3_list, cols)), ACT.Copy)

        def fetch_h_on_vector(m, cols):
            nc.vector.tensor_copy(h_n3[m][:, cols], h_half[m][:].indirect(entries(n3_list, cols)))

        def double(m, cols):
            nc.vector.tensor_scalar(st[m][:, cols], st_neg_half[m][:, cols], -2.0, None, ALU.mult)

        def make_st(m, cols):
            nc.vector.tensor_tensor(st_neg_half[m][:, cols], h_n3[m][:, cols], h_half[m][:, cols], ALU.subtract)

        def finish_on_vector(m, cols):
            nc.vector.tensor_tensor(
                result[m][:, cols], st_neg_half[m][:].indirect(entries(n3_list, cols)), st[m][:, cols], ALU.add
            )
            nc.sync.dma_start(out[blocks[m], cols], result[m][:, cols])

        def finish_with_scalar(m, cols):
            nc.scalar.activation(st[m][:, cols], st_neg_half[m][:].indirect(entries(n3_list, cols)), ACT.Copy)
            nc.vector.scalar_tensor_tensor(
                result[m][:, cols], st_neg_half[m][:, cols], -2.0, st[m][:, cols], ALU.mult, ALU.add
            )
            nc.sync.dma_start(out[blocks[m], cols], result[m][:, cols])

        last = PACK - 1
        evict_d(0, nc.scalar)
        fetch_n2(0, whole)
        nc.vector.tensor_copy(dealt(w1_mx[0]), as_dealt(w1_raw[:]))
        evict_d(1, nc.scalar)
        quantize(w1_mx, whole)
        for t in range(PACK):
            product(y_banks[t][:], w1_mx, blocks[t], offs_words[:], offs_plane[:])
        fetch_n1(0, whole)
        fetch_n2(1, whole)
        evict_d(2, nc.scalar)
        squash(0, whole)
        fetch_n1(1, whole)
        fetch_n2(2, whole)
        make_z(0, whole)
        evict_d(3, nc.scalar)
        squash(1, whole)
        fetch_n1(2, whole)
        fetch_n2(last, first)
        fetch_n2(last, second)
        make_z(1, whole)
        squash(2, whole)
        fetch_n1(last, first)
        fetch_n1(last, second)
        make_z(2, whole)
        squash(last, first)
        squash(last, second)
        w3_mx = mx_tiles("w3", N, ring[(last + 2) % 3])
        weave(nc.scalar.copy, w3_mx[0], w3_raw, first)
        make_z(last, first)
        make_z(last, second)
        weave(nc.scalar.copy, z_mx[0], z_planes, slice(384, S))
        weave(nc.scalar.copy, w3_mx[0], w3_raw, second)
        weave(nc.vector.tensor_copy, z_mx[0], z_planes, first)
        quantize(w3_mx, first)
        quantize(z_mx, first)
        make_h(0, first)
        make_h(1, first)
        weave(nc.vector.tensor_copy, z_mx[0], z_planes, slice(HALF, 384))
        quantize(z_mx, second)
        make_h(0, second)
        make_h(1, second)
        evict_h(0, first)
        evict_h(1, first)
        evict_h_on_vector(0, second)
        quantize(w3_mx, second)
        make_h(2, whole)
        make_h(3, whole)
        evict_h(1, second)
        for cols in halves:
            fetch_h_on_vector(0, cols)
        fetch_h(1, whole)
        for cols in halves:
            make_st(0, cols)
        evict_h(2, whole)
        evict_h(3, whole)
        for cols in halves:
            double(0, cols)
        fetch_h(2, whole)
        fetch_h(3, whole)
        finish_on_vector(0, first)
        make_st(1, whole)
        finish_on_vector(0, second)
        double(1, whole)
        make_st(2, whole)
        finish_on_vector(1, first)
        make_st(3, whole)
        finish_with_scalar(2, whole)
        finish_on_vector(1, second)
        finish_with_scalar(3, first)
        finish_with_scalar(3, second)
